import numpy as np
import ml_dtypes


def mxq(x, axis, fmt="e4m3"):
    dtype, down = {"e4m3": (ml_dtypes.float8_e4m3fn, 7), "e5m2": (ml_dtypes.float8_e5m2, 14)}[fmt]
    v = np.moveaxis(np.asarray(x, np.float32).astype(ml_dtypes.bfloat16).astype(np.float64), axis, -1)
    blocks = v.reshape(v.shape[:-1] + (-1, 32))
    amax = np.abs(blocks).max(-1, keepdims=True)
    byte = np.maximum(np.where(amax > 0, np.frexp(amax)[1] - 1 + 127, 0) - down, 1)
    scale = np.exp2(byte - 127.0)
    codes = (blocks / scale).astype(np.float32).astype(dtype).astype(np.float64)
    return np.moveaxis((codes * scale).reshape(v.shape), -1, axis)


WIDE = False


def mx_kscale(k):
    if not WIDE:
        return np.ones(k)
    levels = np.array([30, -30])
    if k % 512:
        return np.exp2(np.random.permutation(np.resize(levels, k // 32))).repeat(32)
    a = np.empty((k // 512, 16))
    for p in range(k // 512):
        a[p, :8] = np.random.permutation(np.resize(levels, 8))
        for g in range(8):
            far = levels[np.abs(levels - a[p, g]) >= 10]
            a[p, g + 8] = far[np.random.randint(len(far))]
    return np.exp2(a.ravel()).repeat(32)


def f64(x):
    return np.asarray(x).astype(np.float64)


def striped(idx):
    return np.tile(np.asarray(idx).reshape(-1, 16).T, (8, 1)).astype(np.uint16)


def unstriped(offs):
    return offs[:16].T.reshape(-1).astype(np.int64)


E2M1 = np.array([0.0, 0.5, 1.0, 1.5, 2.0, 3.0, 4.0, 6.0, -0.0, -0.5, -1.0, -1.5, -2.0, -3.0, -4.0, -6.0])


def pack_weight(w, fmt):
    k, n = w.shape
    w = f64(np.asarray(w, np.float32).astype(ml_dtypes.bfloat16)).reshape(k // 32, 32, n)
    amax = np.abs(w).max(1)
    if fmt in ("e4m3", "e5m2"):
        byte = np.frexp(amax)[1] - 1 + 127 - (7 if fmt == "e4m3" else 14)
    else:
        mant, ex = np.frexp(amax / 6.0)
        byte = np.where(mant > 0.5, ex, ex - 1) + 127
    byte = np.clip(np.where(amax > 0, byte, 1), 1, 254)
    scaled = (w * np.exp2(127.0 - byte)[:, None, :]).reshape(k, n).astype(np.float32)
    by_word = np.ascontiguousarray(scaled.reshape(k // 512, 128, 4, n).transpose(0, 1, 3, 2))
    if fmt in ("e4m3", "e5m2"):
        words = by_word.astype(ml_dtypes.float8_e4m3fn if fmt == "e4m3" else ml_dtypes.float8_e5m2).view(np.uint8)
    else:
        c = by_word.astype(ml_dtypes.float4_e2m1fn).view(np.uint8) & 0xF
        words = (c[..., 0::2] | (c[..., 1::2] << 4)).reshape(k // 512, 128, 2 * n)
    return np.ascontiguousarray(words), np.ascontiguousarray(byte.astype(np.uint8).reshape(k // 512, 16, n))


def unpack_weight(words, scales, fmt):
    g, _, n = scales.shape
    words = np.ascontiguousarray(words).reshape(g, 128, n, -1)
    if fmt in ("e4m3", "e5m2"):
        vals = words.view(ml_dtypes.float8_e4m3fn if fmt == "e4m3" else ml_dtypes.float8_e5m2).astype(np.float64)
    else:
        nib = np.empty((g, 128, n, 4), np.uint8)
        nib[..., 0::2] = words & 0xF
        nib[..., 1::2] = words >> 4
        vals = E2M1[nib]
    vals = vals * np.repeat(np.exp2(scales.astype(np.float64) - 127.0), 8, axis=1)[..., None]
    return vals.transpose(0, 1, 3, 2).reshape(g * 512, n)


def bf(x):
    return np.asarray(x, np.float32).astype(ml_dtypes.bfloat16)


def planes(Y):
    r, m = Y.shape
    b = f64(bf(Y)).reshape(r // 32, 32, m)
    amax = np.abs(b).max(1)
    byte = np.clip(np.where(amax > 0, np.frexp(amax)[1] - 1 + 127 - 7, 1), 1, 254)
    codes = (b * np.exp2(127.0 - byte)[:, None, :]).reshape(r, m).astype(np.float32).astype(ml_dtypes.float8_e4m3fn).view(np.uint8)
    words = codes.reshape(r // 512, 128, 4, m).transpose(0, 1, 3, 2)
    return np.ascontiguousarray(words), np.ascontiguousarray(byte.astype(np.uint8).reshape(r // 512, 16, m))


K, T, J, R, V, N, Z = 1024, 1024, 384, 512, 512, 512, 512


def setup_inputs():
    n = np.random.standard_normal
    idx = np.random.permutation(T)[:J]
    idx2 = np.random.permutation(V)[:J]
    idx3 = np.random.permutation(Z)[:J]
    fk = mx_kscale(K)
    fr = mx_kscale(R)
    xtp = pack_weight(n((K, T)) / fk[:, None], "e2m1")
    wp = pack_weight(n((K, R)) * 1 / np.sqrt(K) * fk[:, None] * fr, "e5m2")
    wbp = pack_weight(n((R, N)) * 1 / np.sqrt(R) / fr[:, None], "e2m1")
    return {
        "xt_words": xtp[0],
        "xt_scales": xtp[1],
        "w_words": wp[0],
        "w_scales": wp[1],
        "tb": (n((R, V)) * 0.7 * fr[:, None]).astype(np.float32),
        "wb_words": wbp[0],
        "wb_scales": wbp[1],
        "tz": (n((N, Z)) * 0.6).astype(np.float32),
        "rw": (np.random.uniform(0.5, 2.0, (1, J))).astype(np.float32),
        "offs": striped(idx),
        "offs2": striped(idx2),
        "offs3": striped(idx3),
    }


def reference(xt_words, xt_scales, w_words, w_scales, tb, wb_words, wb_scales, tz, rw, offs, offs2, offs3):
    idx = unstriped(offs)
    idx2 = unstriped(offs2)
    idx3 = unstriped(offs3)
    xtu = unpack_weight(xt_words, xt_scales, "e2m1")
    wu = unpack_weight(w_words, w_scales, "e5m2")
    wbu = unpack_weight(wb_words, wb_scales, "e2m1")
    xtidxg = xtu[:, idx]
    a = wu.T @ xtidxg
    hid = np.maximum(a, f64(tb)[:, idx2])
    hidq = mxq(hid, 0, "e4m3")
    p = wbu.T @ hidq
    y = np.maximum(p, f64(tz)[:, idx3]) * f64(rw)
    words, scales = planes(y)
    return y, words, scales

@@ -1,0 +1,258 @@
+from contextlib import ExitStack
+
+import concourse.mybir as mybir
+from concourse.masks import make_identity
+
+K, T, J, R, V, N, Z = 1024, 1024, 384, 512, 512, 512, 512
+FLOPS = 2 * K * R * J + 2 * R * N * J
+
+F32 = mybir.dt.float32
+BF16 = mybir.dt.bfloat16
+I32 = mybir.dt.int32
+U32 = mybir.dt.uint32
+U16 = mybir.dt.uint16
+U8 = mybir.dt.uint8
+E4M3 = mybir.dt.float8_e4m3fn_x4
+E5M2 = mybir.dt.float8_e5m2_x4
+E2M1 = mybir.dt.float4_e2m1fn_x4
+MAX = mybir.AluOpType.max
+MULT = mybir.AluOpType.mult
+COPY = mybir.ActivationFunctionType.Copy
+
+P = 128
+PACK = 4
+PASSES = K // (P * PACK)
+CHUNK = 128
+CHUNKS = J // CHUNK
+GROUP = 16
+FIRST = slice(0, CHUNK)
+REST = slice(CHUNK, J)
+
+
+def listed(offsets, slots):
+    return offsets[:, slots.start // GROUP : slots.stop // GROUP]
+
+
+def by_lines(ap):
+    return ap.rearrange("p t (a i) -> p a t i", i=PACK)
+
+
+def woven_by_lines(ap):
+    return ap.rearrange("p (a i t) -> p a t i", i=PACK, t=PACK)
+
+
+def tile_list_picked_abovetable_floored_pl_kernel(
+    tc, xt_words, xt_scales, w_words, w_scales, tb, wb_words, wb_scales, tz, rw, offs, offs2, offs3, out_0, out_1, out_2
+):
+    nc = tc.nc
+    with ExitStack() as ctx:
+        lists = ctx.enter_context(tc.tile_pool(name="lists", bufs=1))
+        pool = ctx.enter_context(tc.tile_pool(name="pool", bufs=1))
+        psum = ctx.enter_context(tc.psum_pool(name="psum", bufs=1))
+
+        def sbuf(name, columns, dtype):
+            return pool.tile([P, columns], dtype, name=name, align_bytes=64)
+
+        x_list = lists.tile([P, J // GROUP], U16, name="x_list")
+        tb_list = lists.tile([P, J // GROUP], U16, name="tb_list")
+        tz_list = lists.tile([P, J // GROUP], U16, name="tz_list")
+
+        x_words = [sbuf(f"x_words{z}", T, U16) for z in range(PASSES)]
+        x_scales = sbuf("x_scales", PASSES * T, U8)
+        w_raw = sbuf("w_raw", PASSES * R, U32)
+        ws_raw = sbuf("ws_raw", PASSES * R, U8)
+        wb_raw = sbuf("wb_raw", N, U16)
+        wbs_raw = sbuf("wbs_raw", N, U8)
+        tb_low = sbuf("tb_low", 2 * V, F32)
+        tb_high = [sbuf(f"tb_high{t}", V, F32) for t in range(2)]
+        tb_planes = [tb_low[:, :V], tb_low[:, V:], tb_high[0][:], tb_high[1][:]]
+        tz_rows = [sbuf(f"tz_rows{h}", 2 * Z, F32) for h in range(2)]
+        tz_planes = [tz_rows[t // 2][:, (t % 2) * Z : (t % 2 + 1) * Z] for t in range(PACK)]
+        rw_cols = sbuf("rw_cols", CHUNKS, F32)
+        identity = sbuf("identity", P, F32)
+
+        def load_scales(queue, tile, scales):
+            passes = scales.shape[0]
+            for q in range(4):
+                queue.dma_start(
+                    out=tile[32 * q : 32 * q + 4, :].bitcast(I32).rearrange("r (z c) -> r z c", z=passes),
+                    in_=scales[:, 4 * q : 4 * q + 4, :].bitcast(I32).rearrange("z r c -> r z c"),
+                )
+
+        def load_rows(tile, table, first, count):
+            rows = table.rearrange("(p t) v -> p (t v)", t=PACK)
+            nc.sync.dma_start(out=tile[:], in_=rows[:, first * V : (first + count) * V])
+
+        nc.gpsimd.memset(x_scales[:].bitcast(I32), 0)
+        nc.vector.memset(ws_raw[:].bitcast(I32), 0)
+        nc.vector.memset(wbs_raw[:].bitcast(I32), 0)
+
+        nc.sync.dma_start(x_list[:], offs)
+        nc.sync.dma_start(tb_list[:], offs2)
+        load_rows(tb_low, tb, 0, 2)
+        load_scales(nc.scalar, x_scales, xt_scales)
+        nc.sync.dma_start(
+            out=w_raw[:].bitcast(I32).rearrange("p (z c) -> p z c", z=PASSES),
+            in_=w_words.rearrange("z p c b -> p z (c b)").bitcast(I32),
+        )
+        load_scales(nc.sync, ws_raw, w_scales)
+        for z in range(PASSES):
+            nc.sync.dma_start(out=x_words[z][:].bitcast(I32), in_=xt_words[z].bitcast(I32))
+        load_rows(tb_high[0], tb, 2, 1)
+        load_rows(tb_high[1], tb, 3, 1)
+        nc.sync.dma_start(tz_list[:], offs3)
+        nc.sync.dma_start(out=wb_raw[:].bitcast(I32), in_=wb_words[0].bitcast(I32))
+        with nc.allow_non_contiguous_dma(reason="one weight a partition"):
+            nc.sync.dma_start(out=rw_cols[:], in_=rw.rearrange("o (c p) -> p (o c)", p=P))
+        load_rows(tz_rows[0], tz, 0, 2)
+        load_rows(tz_rows[1], tz, 2, 2)
+        make_identity(nc, identity[:])
+        load_scales(nc.gpsimd, wbs_raw, wb_scales)
+
+        xg_words = [sbuf(f"xg_words{z}", J, U16) for z in range(PASSES)]
+        xg_scales = [sbuf(f"xg_scales{z}", J, U8) for z in range(PASSES)]
+        for z in range(PASSES):
+            nc.vector.tensor_copy(xg_scales[z][:], x_scales[:, z * T : (z + 1) * T].indirect(x_list[:]))
+        w_dealt = sbuf("w_dealt", PASSES * R, U32)
+        ws_dealt = sbuf("ws_dealt", PASSES * R, U8)
+        nc.vector.tensor_copy(
+            w_dealt[:].rearrange("p (z t m) -> p z m t", z=PASSES, t=PACK),
+            w_raw[:].rearrange("p (z m t) -> p z m t", z=PASSES, t=PACK),
+        )
+        nc.vector.tensor_copy(
+            ws_dealt[:].rearrange("p (z t m) -> p z m t", z=PASSES, t=PACK),
+            ws_raw[:].rearrange("p (z m t) -> p z m t", z=PASSES, t=PACK),
+        )
+        for slots in (FIRST, REST):
+            for z in range(PASSES):
+                nc.vector.tensor_copy(xg_words[z][:, slots], x_words[z][:].indirect(listed(x_list, slots)))
+
+        tb_picked = sbuf("tb_picked", PACK * J, F32)
+        tz_picked = sbuf("tz_picked", PACK * J, F32)
+
+        def pick(picked, windows, offsets, t, slots, on_vector=False):
+            into = picked[:, t * J + slots.start : t * J + slots.stop]
+            looked_up = windows[t].indirect(listed(offsets, slots))
+            if on_vector:
+                nc.vector.tensor_copy(into, looked_up)
+            else:
+                nc.scalar.activation(into, looked_up, COPY)
+
+        for t in (0, 1):
+            for slots in (FIRST, REST):
+                pick(tb_picked, tb_planes, tb_list, t, slots)
+        for slots in (FIRST, REST):
+            for t in (2, 3):
+                pick(tb_picked, tb_planes, tb_list, t, slots)
+
+        wb_dealt = sbuf("wb_dealt", N, U16)
+        wbs_dealt = sbuf("wbs_dealt", N, U8)
+        nc.vector.tensor_copy(
+            wb_dealt[:].rearrange("p (t m) -> p m t", t=PACK),
+            wb_raw[:].rearrange("p (m t) -> p m t", t=PACK),
+        )
+        nc.gpsimd.tensor_copy(
+            wbs_dealt[:].rearrange("p (t m) -> p t m", t=PACK),
+            wbs_raw[:].rearrange("p (m t) -> p t m", t=PACK),
+        )
+
+        a_banks = [psum.tile([P, PACK, CHUNK], F32, name=f"a_bank{c}") for c in range(CHUNKS)]
+        p_banks = [psum.tile([P, PACK, CHUNK], F32, name=f"p_bank{c}") for c in range(CHUNKS)]
+        rw_bank = psum.tile([P, J], F32, name="rw_bank")
+
+        def chunk_of(picked, c):
+            return picked[:].rearrange("p (t j) -> p t j", t=PACK)[:, :, c * CHUNK : (c + 1) * CHUNK]
+
+        def first_product(c):
+            slots = slice(c * CHUNK, (c + 1) * CHUNK)
+            for t in range(PACK):
+                for z in range(PASSES):
+                    cols = slice(z * R + t * P, z * R + (t + 1) * P)
+                    nc.tensor.matmul_mx(
+                        out=a_banks[c][:, t, :],
+                        lhsT=w_dealt[:, cols].bitcast(E5M2),
+                        lhsT_scale=ws_dealt[:, cols],
+                        rhs=xg_words[z][:, slots].bitcast(E2M1),
+                        rhs_scale=xg_scales[z][:, slots],
+                        start=(z == 0),
+                        stop=(z == PASSES - 1),
+                    )
+
+        hid = [sbuf(f"hid{c}", PACK * CHUNK, BF16) for c in range(CHUNKS)]
+        hid_codes = [sbuf(f"hid_codes{c}", CHUNK, U32) for c in range(CHUNKS)]
+        hid_scales = [sbuf(f"hid_scales{c}", CHUNK, U8) for c in range(CHUNKS)]
+
+        def above_table(c):
+            nc.vector.tensor_tensor(
+                woven_by_lines(hid[c][:]), by_lines(a_banks[c][:]), by_lines(chunk_of(tb_picked, c)), MAX
+            )
+
+        def second_product(c):
+            nc.vector.quantize_mx(out=hid_codes[c][:].bitcast(E4M3), scales=hid_scales[c][:], in_=hid[c][:])
+            for t in range(PACK):
+                nc.tensor.matmul_mx(
+                    out=p_banks[c][:, t, :],
+                    lhsT=wb_dealt[:, t * P : (t + 1) * P].bitcast(E2M1),
+                    lhsT_scale=wbs_dealt[:, t * P : (t + 1) * P],
+                    rhs=hid_codes[c][:].bitcast(E4M3),
+                    rhs_scale=hid_scales[c][:],
+                    start=True,
+                    stop=True,
+                )
+
+        for c in range(CHUNKS):
+            first_product(c)
+        for c in range(CHUNKS):
+            nc.tensor.transpose(
+                rw_bank[:, c * CHUNK : (c + 1) * CHUNK], rw_cols[:, c : c + 1].to_broadcast([P, P]), identity[:]
+            )
+        for c in range(CHUNKS):
+            for t in range(PACK if c == 0 else PACK - 1):
+                pick(tz_picked, tz_planes, tz_list, t, slice(c * CHUNK, (c + 1) * CHUNK))
+        above_table(0)
+        above_table(1)
+        second_product(0)
+        above_table(2)
+        second_product(1)
+        pick(tz_picked, tz_planes, tz_list, PACK - 1, REST, on_vector=True)
+        second_product(2)
+
+        floored = [sbuf(f"floored{c}", PACK * CHUNK, F32) for c in range(CHUNKS)]
+        y = [sbuf(f"y{c}", PACK * CHUNK, F32) for c in range(CHUNKS)]
+        y_woven = [sbuf(f"y_woven{c}", PACK * CHUNK, BF16) for c in range(CHUNKS)]
+        y_codes = sbuf("y_codes", J, U32)
+        y_scales = sbuf("y_scales", J, U8)
+        out_rows = out_0.rearrange("(p t) j -> p t j", t=PACK)
+
+        def planes(tile):
+            return tile[:].rearrange("p (t j) -> p t j", t=PACK)
+
+        def floor(c):
+            nc.vector.tensor_tensor(planes(floored[c]), p_banks[c][:], chunk_of(tz_picked, c), MAX)
+
+        def weigh(c):
+            slots = slice(c * CHUNK, (c + 1) * CHUNK)
+            weights = rw_bank[:, slots].unsqueeze(1).broadcast_to([P, PACK, CHUNK])
+            nc.vector.tensor_tensor(planes(y[c]), planes(floored[c]), weights, MULT)
+            nc.sync.dma_start(out=out_rows[:, :, slots], in_=planes(y[c]))
+            nc.scalar.copy(woven_by_lines(y_woven[c][:]), by_lines(planes(y[c])))
+
+        def hand_on(c):
+            slots = slice(c * CHUNK, (c + 1) * CHUNK)
+            nc.vector.quantize_mx(out=y_codes[:, slots].bitcast(E4M3), scales=y_scales[:, slots], in_=y_woven[c][:])
+
+        floor(0)
+        floor(1)
+        weigh(0)
+        weigh(1)
+        floor(2)
+        hand_on(0)
+        weigh(2)
+        hand_on(1)
+        hand_on(2)
+        nc.sync.dma_start(out=out_1[0].rearrange("p c b -> p (c b)").bitcast(I32), in_=y_codes[:].bitcast(I32))
+        for q in range(4):
+            queue = nc.scalar if q % 2 == 0 else nc.sync
+            queue.dma_start(
+                out=out_2[0, 4 * q : 4 * q + 4, :].bitcast(I32), in_=y_scales[32 * q : 32 * q + 4, :].bitcast(I32)
+            )

@@ -63,9 +63,8 @@ def tile_list_picked_abovetable_floored_pl_kernel(
         ws_raw = sbuf("ws_raw", PASSES * R, U8)
         wb_raw = sbuf("wb_raw", N, U16)
         wbs_raw = sbuf("wbs_raw", N, U8)
-        tb_low = sbuf("tb_low", 2 * V, F32)
-        tb_high = [sbuf(f"tb_high{t}", V, F32) for t in range(2)]
-        tb_planes = [tb_low[:, :V], tb_low[:, V:], tb_high[0][:], tb_high[1][:]]
+        tb_rows = [sbuf(f"tb_rows{h}", 2 * V, F32) for h in range(2)]
+        tb_planes = [tb_rows[t // 2][:, (t % 2) * V : (t % 2 + 1) * V] for t in range(PACK)]
         tz_rows = [sbuf(f"tz_rows{h}", 2 * Z, F32) for h in range(2)]
         tz_planes = [tz_rows[t // 2][:, (t % 2) * Z : (t % 2 + 1) * Z] for t in range(PACK)]
         rw_cols = sbuf("rw_cols", CHUNKS, F32)
@@ -83,49 +82,51 @@ def tile_list_picked_abovetable_floored_pl_kernel(
             rows = table.rearrange("(p t) v -> p (t v)", t=PACK)
             nc.sync.dma_start(out=tile[:], in_=rows[:, first * V : (first + count) * V])
 
+        warm = sbuf("warm", 2, F32)
+        nc.vector.memset(warm[:, 0:1], 0.0)
+        nc.scalar.activation(warm[:, 1:2], warm[:, 0:1], COPY)
         nc.gpsimd.memset(x_scales[:].bitcast(I32), 0)
         nc.vector.memset(ws_raw[:].bitcast(I32), 0)
         nc.vector.memset(wbs_raw[:].bitcast(I32), 0)
+        make_identity(nc, identity[:])
 
         nc.sync.dma_start(x_list[:], offs)
         nc.sync.dma_start(tb_list[:], offs2)
-        load_rows(tb_low, tb, 0, 2)
-        load_scales(nc.scalar, x_scales, xt_scales)
+        load_rows(tb_rows[0], tb, 0, 2)
+        nc.sync.dma_start(out=x_words[0][:].bitcast(I32), in_=xt_words[0].bitcast(I32))
+        load_scales(nc.sync, x_scales, xt_scales)
+        nc.sync.dma_start(out=x_words[1][:].bitcast(I32), in_=xt_words[1].bitcast(I32))
         nc.sync.dma_start(
             out=w_raw[:].bitcast(I32).rearrange("p (z c) -> p z c", z=PASSES),
             in_=w_words.rearrange("z p c b -> p z (c b)").bitcast(I32),
         )
         load_scales(nc.sync, ws_raw, w_scales)
-        for z in range(PASSES):
-            nc.sync.dma_start(out=x_words[z][:].bitcast(I32), in_=xt_words[z].bitcast(I32))
-        load_rows(tb_high[0], tb, 2, 1)
-        load_rows(tb_high[1], tb, 3, 1)
+        load_rows(tb_rows[1], tb, 2, 2)
         nc.sync.dma_start(tz_list[:], offs3)
         nc.sync.dma_start(out=wb_raw[:].bitcast(I32), in_=wb_words[0].bitcast(I32))
-        with nc.allow_non_contiguous_dma(reason="one weight a partition"):
-            nc.sync.dma_start(out=rw_cols[:], in_=rw.rearrange("o (c p) -> p (o c)", p=P))
+        load_scales(nc.sync, wbs_raw, wb_scales)
         load_rows(tz_rows[0], tz, 0, 2)
         load_rows(tz_rows[1], tz, 2, 2)
-        make_identity(nc, identity[:])
-        load_scales(nc.gpsimd, wbs_raw, wb_scales)
+        with nc.allow_non_contiguous_dma(reason="one weight a partition"):
+            nc.sync.dma_start(out=rw_cols[:], in_=rw.rearrange("o (c p) -> p (o c)", p=P))
 
         xg_words = [sbuf(f"xg_words{z}", J, U16) for z in range(PASSES)]
         xg_scales = [sbuf(f"xg_scales{z}", J, U8) for z in range(PASSES)]
-        for z in range(PASSES):
-            nc.vector.tensor_copy(xg_scales[z][:], x_scales[:, z * T : (z + 1) * T].indirect(x_list[:]))
+
+        def pick_tokens(slots):
+            for z in range(PASSES):
+                nc.vector.tensor_copy(xg_words[z][:, slots], x_words[z][:].indirect(listed(x_list, slots)))
+                window = x_scales[:, z * T : (z + 1) * T]
+                nc.vector.tensor_copy(xg_scales[z][:, slots], window.indirect(listed(x_list, slots)))
+
         w_dealt = sbuf("w_dealt", PASSES * R, U32)
         ws_dealt = sbuf("ws_dealt", PASSES * R, U8)
-        nc.vector.tensor_copy(
-            w_dealt[:].rearrange("p (z t m) -> p z m t", z=PASSES, t=PACK),
-            w_raw[:].rearrange("p (z m t) -> p z m t", z=PASSES, t=PACK),
-        )
+        pick_tokens(FIRST)
         nc.vector.tensor_copy(
             ws_dealt[:].rearrange("p (z t m) -> p z m t", z=PASSES, t=PACK),
             ws_raw[:].rearrange("p (z m t) -> p z m t", z=PASSES, t=PACK),
         )
-        for slots in (FIRST, REST):
-            for z in range(PASSES):
-                nc.vector.tensor_copy(xg_words[z][:, slots], x_words[z][:].indirect(listed(x_list, slots)))
+        pick_tokens(REST)
 
         tb_picked = sbuf("tb_picked", PACK * J, F32)
         tz_picked = sbuf("tz_picked", PACK * J, F32)
@@ -141,6 +142,10 @@ def tile_list_picked_abovetable_floored_pl_kernel(
         for t in (0, 1):
             for slots in (FIRST, REST):
                 pick(tb_picked, tb_planes, tb_list, t, slots)
+        nc.scalar.copy(
+            w_dealt[:].rearrange("p (z t m) -> p z m t", z=PASSES, t=PACK),
+            w_raw[:].rearrange("p (z m t) -> p z m t", z=PASSES, t=PACK),
+        )
         for slots in (FIRST, REST):
             for t in (2, 3):
                 pick(tb_picked, tb_planes, tb_list, t, slots)
@@ -151,9 +156,9 @@ def tile_list_picked_abovetable_floored_pl_kernel(
             wb_dealt[:].rearrange("p (t m) -> p m t", t=PACK),
             wb_raw[:].rearrange("p (m t) -> p m t", t=PACK),
         )
-        nc.gpsimd.tensor_copy(
-            wbs_dealt[:].rearrange("p (t m) -> p t m", t=PACK),
-            wbs_raw[:].rearrange("p (m t) -> p t m", t=PACK),
+        nc.vector.tensor_copy(
+            wbs_dealt[:].rearrange("p (t m) -> p m t", t=PACK),
+            wbs_raw[:].rearrange("p (m t) -> p m t", t=PACK),
         )
 
         a_banks = [psum.tile([P, PACK, CHUNK], F32, name=f"a_bank{c}") for c in range(CHUNKS)]
@@ -207,14 +212,13 @@ def tile_list_picked_abovetable_floored_pl_kernel(
                 rw_bank[:, c * CHUNK : (c + 1) * CHUNK], rw_cols[:, c : c + 1].to_broadcast([P, P]), identity[:]
             )
         for c in range(CHUNKS):
-            for t in range(PACK if c == 0 else PACK - 1):
+            for t in range(PACK):
                 pick(tz_picked, tz_planes, tz_list, t, slice(c * CHUNK, (c + 1) * CHUNK))
         above_table(0)
         above_table(1)
         second_product(0)
         above_table(2)
         second_product(1)
-        pick(tz_picked, tz_planes, tz_list, PACK - 1, REST, on_vector=True)
         second_product(2)
 
         floored = [sbuf(f"floored{c}", PACK * CHUNK, F32) for c in range(CHUNKS)]

@@ -50,8 +50,8 @@ def tile_list_picked_abovetable_floored_pl_kernel(
         pool = ctx.enter_context(tc.tile_pool(name="pool", bufs=1))
         psum = ctx.enter_context(tc.psum_pool(name="psum", bufs=1))
 
-        def sbuf(name, columns, dtype):
-            return pool.tile([P, columns], dtype, name=name, align_bytes=64)
+        def sbuf(name, columns, dtype, tag=None):
+            return pool.tile([P, columns], dtype, name=name, tag=tag or name, align_bytes=64)
 
         x_list = lists.tile([P, J // GROUP], U16, name="x_list")
         tb_list = lists.tile([P, J // GROUP], U16, name="tb_list")
@@ -82,51 +82,57 @@ def tile_list_picked_abovetable_floored_pl_kernel(
             rows = table.rearrange("(p t) v -> p (t v)", t=PACK)
             nc.sync.dma_start(out=tile[:], in_=rows[:, first * V : (first + count) * V])
 
-        warm = sbuf("warm", 2, F32)
-        nc.vector.memset(warm[:, 0:1], 0.0)
-        nc.scalar.activation(warm[:, 1:2], warm[:, 0:1], COPY)
-        nc.gpsimd.memset(x_scales[:].bitcast(I32), 0)
-        nc.vector.memset(ws_raw[:].bitcast(I32), 0)
+        nc.gpsimd.memset(ws_raw[:].bitcast(I32), 0)
+        nc.vector.memset(x_scales[:].bitcast(I32), 0)
         nc.vector.memset(wbs_raw[:].bitcast(I32), 0)
-        make_identity(nc, identity[:])
 
         nc.sync.dma_start(x_list[:], offs)
+        nc.scalar.dma_start(out=wb_raw[:].bitcast(I32), in_=wb_words[0].bitcast(I32))
         nc.sync.dma_start(tb_list[:], offs2)
-        load_rows(tb_rows[0], tb, 0, 2)
         nc.sync.dma_start(out=x_words[0][:].bitcast(I32), in_=xt_words[0].bitcast(I32))
-        load_scales(nc.sync, x_scales, xt_scales)
+        load_rows(tb_rows[0], tb, 0, 2)
+        load_scales(nc.sync, ws_raw, w_scales)
         nc.sync.dma_start(out=x_words[1][:].bitcast(I32), in_=xt_words[1].bitcast(I32))
         nc.sync.dma_start(
             out=w_raw[:].bitcast(I32).rearrange("p (z c) -> p z c", z=PASSES),
             in_=w_words.rearrange("z p c b -> p z (c b)").bitcast(I32),
         )
-        load_scales(nc.sync, ws_raw, w_scales)
+        load_scales(nc.sync, x_scales, xt_scales)
         load_rows(tb_rows[1], tb, 2, 2)
-        nc.sync.dma_start(tz_list[:], offs3)
-        nc.sync.dma_start(out=wb_raw[:].bitcast(I32), in_=wb_words[0].bitcast(I32))
-        load_scales(nc.sync, wbs_raw, wb_scales)
         load_rows(tz_rows[0], tz, 0, 2)
+        nc.sync.dma_start(tz_list[:], offs3)
+        load_scales(nc.sync, wbs_raw, wb_scales)
         load_rows(tz_rows[1], tz, 2, 2)
         with nc.allow_non_contiguous_dma(reason="one weight a partition"):
             nc.sync.dma_start(out=rw_cols[:], in_=rw.rearrange("o (c p) -> p (o c)", p=P))
 
+        make_identity(nc, identity[:])
+
         xg_words = [sbuf(f"xg_words{z}", J, U16) for z in range(PASSES)]
         xg_scales = [sbuf(f"xg_scales{z}", J, U8) for z in range(PASSES)]
 
-        def pick_tokens(slots):
-            for z in range(PASSES):
-                nc.vector.tensor_copy(xg_words[z][:, slots], x_words[z][:].indirect(listed(x_list, slots)))
+        def pick_words(z):
+            nc.vector.tensor_copy(xg_words[z][:], x_words[z][:].indirect(x_list[:]))
+
+        def pick_scales(z):
+            for slots in (FIRST, REST):
                 window = x_scales[:, z * T : (z + 1) * T]
                 nc.vector.tensor_copy(xg_scales[z][:, slots], window.indirect(listed(x_list, slots)))
 
         w_dealt = sbuf("w_dealt", PASSES * R, U32)
-        ws_dealt = sbuf("ws_dealt", PASSES * R, U8)
-        pick_tokens(FIRST)
+        ws_dealt = sbuf("ws_dealt", PASSES * R, U8, tag="x_words0")
+        pick_words(0)
         nc.vector.tensor_copy(
             ws_dealt[:].rearrange("p (z t m) -> p z m t", z=PASSES, t=PACK),
             ws_raw[:].rearrange("p (z m t) -> p z m t", z=PASSES, t=PACK),
         )
-        pick_tokens(REST)
+        pick_words(1)
+        nc.vector.tensor_copy(
+            w_dealt[:].rearrange("p (z t m) -> p z m t", z=PASSES, t=PACK),
+            w_raw[:].rearrange("p (z m t) -> p z m t", z=PASSES, t=PACK),
+        )
+        pick_scales(0)
+        pick_scales(1)
 
         tb_picked = sbuf("tb_picked", PACK * J, F32)
         tz_picked = sbuf("tz_picked", PACK * J, F32)
@@ -142,36 +148,31 @@ def tile_list_picked_abovetable_floored_pl_kernel(
         for t in (0, 1):
             for slots in (FIRST, REST):
                 pick(tb_picked, tb_planes, tb_list, t, slots)
-        nc.scalar.copy(
-            w_dealt[:].rearrange("p (z t m) -> p z m t", z=PASSES, t=PACK),
-            w_raw[:].rearrange("p (z m t) -> p z m t", z=PASSES, t=PACK),
-        )
         for slots in (FIRST, REST):
             for t in (2, 3):
-                pick(tb_picked, tb_planes, tb_list, t, slots)
+                pick(tb_picked, tb_planes, tb_list, t, slots, on_vector=(t == 3 and slots is REST))
 
         wb_dealt = sbuf("wb_dealt", N, U16)
         wbs_dealt = sbuf("wbs_dealt", N, U8)
-        nc.vector.tensor_copy(
+        nc.scalar.copy(
             wb_dealt[:].rearrange("p (t m) -> p m t", t=PACK),
             wb_raw[:].rearrange("p (m t) -> p m t", t=PACK),
         )
-        nc.vector.tensor_copy(
-            wbs_dealt[:].rearrange("p (t m) -> p m t", t=PACK),
-            wbs_raw[:].rearrange("p (m t) -> p m t", t=PACK),
+        nc.gpsimd.tensor_copy(
+            wbs_dealt[:].rearrange("p (t m) -> p t m", t=PACK),
+            wbs_raw[:].rearrange("p (m t) -> p t m", t=PACK),
         )
 
         a_banks = [psum.tile([P, PACK, CHUNK], F32, name=f"a_bank{c}") for c in range(CHUNKS)]
-        p_banks = [psum.tile([P, PACK, CHUNK], F32, name=f"p_bank{c}") for c in range(CHUNKS)]
         rw_bank = psum.tile([P, J], F32, name="rw_bank")
 
         def chunk_of(picked, c):
             return picked[:].rearrange("p (t j) -> p t j", t=PACK)[:, :, c * CHUNK : (c + 1) * CHUNK]
 
-        def first_product(c):
-            slots = slice(c * CHUNK, (c + 1) * CHUNK)
-            for t in range(PACK):
-                for z in range(PASSES):
+        def first_product(z):
+            for c in range(CHUNKS):
+                slots = slice(c * CHUNK, (c + 1) * CHUNK)
+                for t in range(PACK):
                     cols = slice(z * R + t * P, z * R + (t + 1) * P)
                     nc.tensor.matmul_mx(
                         out=a_banks[c][:, t, :],
@@ -179,8 +180,8 @@ def tile_list_picked_abovetable_floored_pl_kernel(
                         lhsT_scale=ws_dealt[:, cols],
                         rhs=xg_words[z][:, slots].bitcast(E2M1),
                         rhs_scale=xg_scales[z][:, slots],
-                        start=(z == 0),
-                        stop=(z == PASSES - 1),
+                        start=(z == 0 and t == 0),
+                        stop=(z == PASSES - 1 and t == PACK - 1),
                     )
 
         hid = [sbuf(f"hid{c}", PACK * CHUNK, BF16) for c in range(CHUNKS)]
@@ -192,8 +193,13 @@ def tile_list_picked_abovetable_floored_pl_kernel(
                 woven_by_lines(hid[c][:]), by_lines(a_banks[c][:]), by_lines(chunk_of(tb_picked, c)), MAX
             )
 
-        def second_product(c):
+        def quantise_hid(c):
             nc.vector.quantize_mx(out=hid_codes[c][:].bitcast(E4M3), scales=hid_scales[c][:], in_=hid[c][:])
+
+        p_banks = []
+
+        def second_product(c):
+            p_banks.append(psum.tile([P, PACK, CHUNK], F32, name=f"p_bank{c}"))
             for t in range(PACK):
                 nc.tensor.matmul_mx(
                     out=p_banks[c][:, t, :],
@@ -205,8 +211,8 @@ def tile_list_picked_abovetable_floored_pl_kernel(
                     stop=True,
                 )
 
-        for c in range(CHUNKS):
-            first_product(c)
+        for z in range(PASSES):
+            first_product(z)
         for c in range(CHUNKS):
             nc.tensor.transpose(
                 rw_bank[:, c * CHUNK : (c + 1) * CHUNK], rw_cols[:, c : c + 1].to_broadcast([P, P]), identity[:]
@@ -216,10 +222,12 @@ def tile_list_picked_abovetable_floored_pl_kernel(
                 pick(tz_picked, tz_planes, tz_list, t, slice(c * CHUNK, (c + 1) * CHUNK))
         above_table(0)
         above_table(1)
-        second_product(0)
+        quantise_hid(0)
         above_table(2)
-        second_product(1)
-        second_product(2)
+        quantise_hid(1)
+        quantise_hid(2)
+        for c in range(CHUNKS):
+            second_product(c)
 
         floored = [sbuf(f"floored{c}", PACK * CHUNK, F32) for c in range(CHUNKS)]
         y = [sbuf(f"y{c}", PACK * CHUNK, F32) for c in range(CHUNKS)]
@@ -239,22 +247,29 @@ def tile_list_picked_abovetable_floored_pl_kernel(
             weights = rw_bank[:, slots].unsqueeze(1).broadcast_to([P, PACK, CHUNK])
             nc.vector.tensor_tensor(planes(y[c]), planes(floored[c]), weights, MULT)
             nc.sync.dma_start(out=out_rows[:, :, slots], in_=planes(y[c]))
-            nc.scalar.copy(woven_by_lines(y_woven[c][:]), by_lines(planes(y[c])))
+
+        def weave(c, copy):
+            copy(woven_by_lines(y_woven[c][:]), by_lines(planes(y[c])))
 
         def hand_on(c):
             slots = slice(c * CHUNK, (c + 1) * CHUNK)
             nc.vector.quantize_mx(out=y_codes[:, slots].bitcast(E4M3), scales=y_scales[:, slots], in_=y_woven[c][:])
 
+        out_words = out_1[0].rearrange("p c b -> p (c b)").bitcast(I32)
         floor(0)
         floor(1)
         weigh(0)
-        weigh(1)
+        weave(0, nc.scalar.copy)
         floor(2)
-        hand_on(0)
+        weigh(1)
+        weave(1, nc.scalar.copy)
         weigh(2)
+        hand_on(0)
+        weave(2, nc.vector.tensor_copy)
         hand_on(1)
+        nc.sync.dma_start(out=out_words[:, : 2 * CHUNK], in_=y_codes[:, : 2 * CHUNK].bitcast(I32))
         hand_on(2)
-        nc.sync.dma_start(out=out_1[0].rearrange("p c b -> p (c b)").bitcast(I32), in_=y_codes[:].bitcast(I32))
+        nc.sync.dma_start(out=out_words[:, 2 * CHUNK :], in_=y_codes[:, 2 * CHUNK :].bitcast(I32))
         for q in range(4):
             queue = nc.scalar if q % 2 == 0 else nc.sync
             queue.dma_start(

from contextlib import ExitStack

import concourse.mybir as mybir
from concourse.masks import make_identity

K, T, J, R, V, N, Z = 1024, 1024, 384, 512, 512, 512, 512
FLOPS = 2 * K * R * J + 2 * R * N * J

F32 = mybir.dt.float32
BF16 = mybir.dt.bfloat16
I32 = mybir.dt.int32
U32 = mybir.dt.uint32
U16 = mybir.dt.uint16
U8 = mybir.dt.uint8
E4M3 = mybir.dt.float8_e4m3fn_x4
E5M2 = mybir.dt.float8_e5m2_x4
E2M1 = mybir.dt.float4_e2m1fn_x4
MAX = mybir.AluOpType.max
MULT = mybir.AluOpType.mult
COPY = mybir.ActivationFunctionType.Copy

P = 128
PACK = 4
PASSES = K // (P * PACK)
CHUNK = 128
CHUNKS = J // CHUNK
GROUP = 16
FIRST = slice(0, CHUNK)
REST = slice(CHUNK, J)


def listed(offsets, slots):
    return offsets[:, slots.start // GROUP : slots.stop // GROUP]


def by_lines(ap):
    return ap.rearrange("p t (a i) -> p a t i", i=PACK)


def woven_by_lines(ap):
    return ap.rearrange("p (a i t) -> p a t i", i=PACK, t=PACK)


def tile_list_picked_abovetable_floored_pl_kernel(
    tc, xt_words, xt_scales, w_words, w_scales, tb, wb_words, wb_scales, tz, rw, offs, offs2, offs3, out_0, out_1, out_2
):
    nc = tc.nc
    with ExitStack() as ctx:
        lists = ctx.enter_context(tc.tile_pool(name="lists", bufs=1))
        pool = ctx.enter_context(tc.tile_pool(name="pool", bufs=1))
        psum = ctx.enter_context(tc.psum_pool(name="psum", bufs=1))

        def sbuf(name, columns, dtype, tag=None):
            return pool.tile([P, columns], dtype, name=name, tag=tag or name, align_bytes=64)

        x_list = lists.tile([P, J // GROUP], U16, name="x_list")
        tb_list = lists.tile([P, J // GROUP], U16, name="tb_list")
        tz_list = lists.tile([P, J // GROUP], U16, name="tz_list")

        x_words = [sbuf(f"x_words{z}", T, U16) for z in range(PASSES)]
        x_scales = sbuf("x_scales", PASSES * T, U8)
        w_raw = sbuf("w_raw", PASSES * R, U32)
        ws_raw = sbuf("ws_raw", PASSES * R, U8)
        wb_raw = sbuf("wb_raw", N, U16)
        wbs_raw = sbuf("wbs_raw", N, U8)
        tb_rows = [sbuf(f"tb_rows{h}", 2 * V, F32) for h in range(2)]
        tb_planes = [tb_rows[t // 2][:, (t % 2) * V : (t % 2 + 1) * V] for t in range(PACK)]
        tz_rows = [sbuf(f"tz_rows{h}", 2 * Z, F32) for h in range(2)]
        tz_planes = [tz_rows[t // 2][:, (t % 2) * Z : (t % 2 + 1) * Z] for t in range(PACK)]
        rw_cols = sbuf("rw_cols", CHUNKS, F32)
        identity = sbuf("identity", P, F32)

        def load_scales(queue, tile, scales):
            passes = scales.shape[0]
            for q in range(4):
                queue.dma_start(
                    out=tile[32 * q : 32 * q + 4, :].bitcast(I32).rearrange("r (z c) -> r z c", z=passes),
                    in_=scales[:, 4 * q : 4 * q + 4, :].bitcast(I32).rearrange("z r c -> r z c"),
                )

        def load_rows(tile, table, first, count):
            rows = table.rearrange("(p t) v -> p (t v)", t=PACK)
            nc.sync.dma_start(out=tile[:], in_=rows[:, first * V : (first + count) * V])

        nc.gpsimd.memset(ws_raw[:].bitcast(I32), 0)
        nc.vector.memset(x_scales[:].bitcast(I32), 0)
        nc.vector.memset(wbs_raw[:].bitcast(I32), 0)

        nc.sync.dma_start(x_list[:], offs)
        nc.scalar.dma_start(out=wb_raw[:].bitcast(I32), in_=wb_words[0].bitcast(I32))
        nc.sync.dma_start(tb_list[:], offs2)
        nc.sync.dma_start(out=x_words[0][:].bitcast(I32), in_=xt_words[0].bitcast(I32))
        load_rows(tb_rows[0], tb, 0, 2)
        load_scales(nc.sync, ws_raw, w_scales)
        nc.sync.dma_start(out=x_words[1][:].bitcast(I32), in_=xt_words[1].bitcast(I32))
        nc.sync.dma_start(
            out=w_raw[:].bitcast(I32).rearrange("p (z c) -> p z c", z=PASSES),
            in_=w_words.rearrange("z p c b -> p z (c b)").bitcast(I32),
        )
        load_scales(nc.sync, x_scales, xt_scales)
        load_rows(tb_rows[1], tb, 2, 2)
        load_rows(tz_rows[0], tz, 0, 2)
        nc.sync.dma_start(tz_list[:], offs3)
        load_scales(nc.sync, wbs_raw, wb_scales)
        load_rows(tz_rows[1], tz, 2, 2)
        with nc.allow_non_contiguous_dma(reason="one weight a partition"):
            nc.sync.dma_start(out=rw_cols[:], in_=rw.rearrange("o (c p) -> p (o c)", p=P))

        make_identity(nc, identity[:])

        xg_words = [sbuf(f"xg_words{z}", J, U16) for z in range(PASSES)]
        xg_scales = [sbuf(f"xg_scales{z}", J, U8) for z in range(PASSES)]

        def pick_words(z):
            nc.vector.tensor_copy(xg_words[z][:], x_words[z][:].indirect(x_list[:]))

        def pick_scales(z):
            for slots in (FIRST, REST):
                window = x_scales[:, z * T : (z + 1) * T]
                nc.vector.tensor_copy(xg_scales[z][:, slots], window.indirect(listed(x_list, slots)))

        w_dealt = sbuf("w_dealt", PASSES * R, U32)
        ws_dealt = sbuf("ws_dealt", PASSES * R, U8, tag="x_words0")
        pick_words(0)
        nc.vector.tensor_copy(
            ws_dealt[:].rearrange("p (z t m) -> p z m t", z=PASSES, t=PACK),
            ws_raw[:].rearrange("p (z m t) -> p z m t", z=PASSES, t=PACK),
        )
        pick_words(1)
        nc.vector.tensor_copy(
            w_dealt[:].rearrange("p (z t m) -> p z m t", z=PASSES, t=PACK),
            w_raw[:].rearrange("p (z m t) -> p z m t", z=PASSES, t=PACK),
        )
        pick_scales(0)
        pick_scales(1)

        tb_picked = sbuf("tb_picked", PACK * J, F32)
        tz_picked = sbuf("tz_picked", PACK * J, F32)

        def pick(picked, windows, offsets, t, slots, on_vector=False):
            into = picked[:, t * J + slots.start : t * J + slots.stop]
            looked_up = windows[t].indirect(listed(offsets, slots))
            if on_vector:
                nc.vector.tensor_copy(into, looked_up)
            else:
                nc.scalar.activation(into, looked_up, COPY)

        for t in (0, 1):
            for slots in (FIRST, REST):
                pick(tb_picked, tb_planes, tb_list, t, slots)
        for slots in (FIRST, REST):
            for t in (2, 3):
                pick(tb_picked, tb_planes, tb_list, t, slots, on_vector=(t == 3 and slots is REST))

        wb_dealt = sbuf("wb_dealt", N, U16)
        wbs_dealt = sbuf("wbs_dealt", N, U8)
        nc.scalar.copy(
            wb_dealt[:].rearrange("p (t m) -> p m t", t=PACK),
            wb_raw[:].rearrange("p (m t) -> p m t", t=PACK),
        )
        nc.gpsimd.tensor_copy(
            wbs_dealt[:].rearrange("p (t m) -> p t m", t=PACK),
            wbs_raw[:].rearrange("p (m t) -> p t m", t=PACK),
        )

        a_banks = [psum.tile([P, PACK, CHUNK], F32, name=f"a_bank{c}") for c in range(CHUNKS)]
        rw_bank = psum.tile([P, J], F32, name="rw_bank")

        def chunk_of(picked, c):
            return picked[:].rearrange("p (t j) -> p t j", t=PACK)[:, :, c * CHUNK : (c + 1) * CHUNK]

        def first_product(z):
            for c in range(CHUNKS):
                slots = slice(c * CHUNK, (c + 1) * CHUNK)
                for t in range(PACK):
                    cols = slice(z * R + t * P, z * R + (t + 1) * P)
                    nc.tensor.matmul_mx(
                        out=a_banks[c][:, t, :],
                        lhsT=w_dealt[:, cols].bitcast(E5M2),
                        lhsT_scale=ws_dealt[:, cols],
                        rhs=xg_words[z][:, slots].bitcast(E2M1),
                        rhs_scale=xg_scales[z][:, slots],
                        start=(z == 0 and t == 0),
                        stop=(z == PASSES - 1 and t == PACK - 1),
                    )

        hid = [sbuf(f"hid{c}", PACK * CHUNK, BF16) for c in range(CHUNKS)]
        hid_codes = [sbuf(f"hid_codes{c}", CHUNK, U32) for c in range(CHUNKS)]
        hid_scales = [sbuf(f"hid_scales{c}", CHUNK, U8) for c in range(CHUNKS)]

        def above_table(c):
            nc.vector.tensor_tensor(
                woven_by_lines(hid[c][:]), by_lines(a_banks[c][:]), by_lines(chunk_of(tb_picked, c)), MAX
            )

        def quantise_hid(c):
            nc.vector.quantize_mx(out=hid_codes[c][:].bitcast(E4M3), scales=hid_scales[c][:], in_=hid[c][:])

        p_banks = []

        def second_product(c):
            p_banks.append(psum.tile([P, PACK, CHUNK], F32, name=f"p_bank{c}"))
            for t in range(PACK):
                nc.tensor.matmul_mx(
                    out=p_banks[c][:, t, :],
                    lhsT=wb_dealt[:, t * P : (t + 1) * P].bitcast(E2M1),
                    lhsT_scale=wbs_dealt[:, t * P : (t + 1) * P],
                    rhs=hid_codes[c][:].bitcast(E4M3),
                    rhs_scale=hid_scales[c][:],
                    start=True,
                    stop=True,
                )

        for z in range(PASSES):
            first_product(z)
        for c in range(CHUNKS):
            nc.tensor.transpose(
                rw_bank[:, c * CHUNK : (c + 1) * CHUNK], rw_cols[:, c : c + 1].to_broadcast([P, P]), identity[:]
            )
        for c in range(CHUNKS):
            for t in range(PACK):
                pick(tz_picked, tz_planes, tz_list, t, slice(c * CHUNK, (c + 1) * CHUNK))
        above_table(0)
        above_table(1)
        quantise_hid(0)
        above_table(2)
        quantise_hid(1)
        quantise_hid(2)
        for c in range(CHUNKS):
            second_product(c)

        floored = [sbuf(f"floored{c}", PACK * CHUNK, F32) for c in range(CHUNKS)]
        y = [sbuf(f"y{c}", PACK * CHUNK, F32) for c in range(CHUNKS)]
        y_woven = [sbuf(f"y_woven{c}", PACK * CHUNK, BF16) for c in range(CHUNKS)]
        y_codes = sbuf("y_codes", J, U32)
        y_scales = sbuf("y_scales", J, U8)
        out_rows = out_0.rearrange("(p t) j -> p t j", t=PACK)

        def planes(tile):
            return tile[:].rearrange("p (t j) -> p t j", t=PACK)

        def floor(c):
            nc.vector.tensor_tensor(planes(floored[c]), p_banks[c][:], chunk_of(tz_picked, c), MAX)

        def weigh(c):
            slots = slice(c * CHUNK, (c + 1) * CHUNK)
            weights = rw_bank[:, slots].unsqueeze(1).broadcast_to([P, PACK, CHUNK])
            nc.vector.tensor_tensor(planes(y[c]), planes(floored[c]), weights, MULT)
            nc.sync.dma_start(out=out_rows[:, :, slots], in_=planes(y[c]))

        def weave(c, copy):
            copy(woven_by_lines(y_woven[c][:]), by_lines(planes(y[c])))

        def hand_on(c):
            slots = slice(c * CHUNK, (c + 1) * CHUNK)
            nc.vector.quantize_mx(out=y_codes[:, slots].bitcast(E4M3), scales=y_scales[:, slots], in_=y_woven[c][:])

        out_words = out_1[0].rearrange("p c b -> p (c b)").bitcast(I32)
        floor(0)
        floor(1)
        weigh(0)
        weave(0, nc.scalar.copy)
        floor(2)
        weigh(1)
        weave(1, nc.scalar.copy)
        weigh(2)
        hand_on(0)
        weave(2, nc.vector.tensor_copy)
        hand_on(1)
        nc.sync.dma_start(out=out_words[:, : 2 * CHUNK], in_=y_codes[:, : 2 * CHUNK].bitcast(I32))
        hand_on(2)
        nc.sync.dma_start(out=out_words[:, 2 * CHUNK :], in_=y_codes[:, 2 * CHUNK :].bitcast(I32))
        for q in range(4):
            queue = nc.scalar if q % 2 == 0 else nc.sync
            queue.dma_start(
                out=out_2[0, 4 * q : 4 * q + 4, :].bitcast(I32), in_=y_scales[32 * q : 32 * q + 4, :].bitcast(I32)
            )
